import numpy as np
import ml_dtypes


def mxq(x, axis, fmt="e4m3"):
    dtype, down = {"e4m3": (ml_dtypes.float8_e4m3fn, 7), "e5m2": (ml_dtypes.float8_e5m2, 14)}[fmt]
    v = np.moveaxis(np.asarray(x, np.float32).astype(ml_dtypes.bfloat16).astype(np.float64), axis, -1)
    blocks = v.reshape(v.shape[:-1] + (-1, 32))
    amax = np.abs(blocks).max(-1, keepdims=True)
    byte = np.maximum(np.where(amax > 0, np.frexp(amax)[1] - 1 + 127, 0) - down, 1)
    scale = np.exp2(byte - 127.0)
    codes = (blocks / scale).astype(np.float32).astype(dtype).astype(np.float64)
    return np.moveaxis((codes * scale).reshape(v.shape), -1, axis)


WIDE = False


def mx_kscale(k):
    if not WIDE:
        return np.ones(k)
    levels = np.array([10, -10, 5, -5, 0])
    if k % 512:
        return np.exp2(np.random.permutation(np.resize(levels, k // 32))).repeat(32)
    a = np.empty((k // 512, 16))
    for p in range(k // 512):
        a[p, :8] = np.random.permutation(np.resize(levels, 8))
        for g in range(8):
            far = levels[np.abs(levels - a[p, g]) >= 10]
            a[p, g + 8] = far[np.random.randint(len(far))]
    return np.exp2(a.ravel()).repeat(32)


def f64(x):
    return np.asarray(x).astype(np.float64)


def striped(idx):
    return np.tile(idx.reshape(-1, 16).T, (8, 1)).astype(np.uint16)


def unstriped(offs):
    return offs[:16].T.reshape(-1).astype(np.int64)


def pack_weight(w):
    k, n = w.shape
    w = f64(np.asarray(w, np.float32).astype(ml_dtypes.bfloat16)).reshape(k // 32, 32, n)
    amax = np.abs(w).max(1)
    byte = np.clip(np.where(amax > 0, np.frexp(amax)[1] - 1 + 127 - 7, 1), 1, 254)
    scaled = (w * np.exp2(127.0 - byte)[:, None, :]).reshape(k, n).astype(np.float32)
    words = np.ascontiguousarray(scaled.reshape(k // 512, 128, 4, n).transpose(0, 1, 3, 2)).astype(ml_dtypes.float8_e4m3fn).view(np.uint8)
    return words, np.ascontiguousarray(byte.astype(np.uint8).reshape(k // 512, 16, n))


def unpack_weight(words, scales):
    g, p, n, _ = words.shape
    vals = np.ascontiguousarray(words).view(ml_dtypes.float8_e4m3fn).astype(np.float64) * np.repeat(np.exp2(scales.astype(np.float64) - 127.0), 8, axis=1)[..., None]
    return vals.transpose(0, 1, 3, 2).reshape(g * 512, n)


def relu(v):
    return np.maximum(v, 0.0)


K, T, S, D, N, V = 512, 4096, 1024, 4, 256, 256


def setup_inputs():
    n = np.random.standard_normal
    s = mx_kscale(K)[:, None]
    packed_xT = pack_weight(n((K, T)) * s)
    return {
        "x_words": packed_xT[0],
        "x_scales": packed_xT[1],
        "w1": (n((K, N)) / np.sqrt(K) / s).astype(np.float32),
        "w2": (n((K, N)) / np.sqrt(K) / s).astype(np.float32),
        "unom": (n((N, V))).astype(np.float32),
        "offs": striped(np.random.permutation(T)[:S]),
    }


def reference(x_words, x_scales, w1, w2, unom, offs):
    xq = unpack_weight(x_words, x_scales)[:, unstriped(offs)]
    yg = mxq(f64(w2), 0, "e4m3").T @ xq
    yh = mxq(f64(w1), 0, "e4m3").T @ xq
    bar = np.exp(0.4 * yh)
    slack = yg * (np.repeat(f64(unom), D, axis=1)) + 0.8 * (bar - 1.0)
    wst = slack.reshape(len(slack), -1, D).min(axis=2)
    ws = np.exp(5.0 * (np.repeat(wst, D, axis=1) - slack))
    mult = relu(-1.0 * slack) / ((yg) ** 2 + 0.3)
    wk = (ws * mult) * yg
    return f64(unom) + (wk.reshape(len(wk), -1, D).sum(axis=2)) / (ws.reshape(len(ws), -1, D).sum(axis=2))

@@ -1,0 +1,147 @@
+from contextlib import ExitStack
+
+import concourse.mybir as mybir
+from concourse.masks import make_identity
+
+F32 = mybir.dt.float32
+BF16 = mybir.dt.bfloat16
+I32 = mybir.dt.int32
+U32 = mybir.dt.uint32
+U16 = mybir.dt.uint16
+U8 = mybir.dt.uint8
+FP8X4 = mybir.dt.float8_e4m3fn_x4
+ALU = mybir.AluOpType
+ACT = mybir.ActivationFunctionType
+
+P = 128
+K, T, S, D, M, V = 512, 4096, 1024, 4, 256, 256
+HALVES = 2
+CHUNK = D * P
+FLOPS = 2 * 2 * K * M * S
+SHRINK = 2.0 ** -24
+
+
+def tile_picked_ycbf_worst_p_kernel(tc, x_words, x_scales, w1, w2, unom, offs, out):
+    nc = tc.nc
+    chunks = [(vb, mh) for vb in range(HALVES) for mh in range(HALVES)]
+    n_chunks = len(chunks)
+    with ExitStack() as ctx:
+        keep = ctx.enter_context(tc.tile_pool(name="keep", bufs=1))
+        psum = ctx.enter_context(tc.psum_pool(name="psum", bufs=1))
+
+        offsets = keep.tile([P, S // 16], U16, name="offsets")
+        nc.sync.dma_start(offsets[:], offs)
+        u_rows = keep.tile([P, HALVES, V], F32, name="u_rows")
+        nc.sync.dma_start(u_rows[:], unom.rearrange("(h p) v -> p h v", p=P))
+        table_words = keep.tile([P, T], U32, name="table_words", align_bytes=64)
+        nc.sync.dma_start(table_words[:].bitcast(I32), x_words[0].rearrange("p n t -> p (n t)").bitcast(I32))
+        raw = {}
+        for name, w in (("g", w2), ("h", w1)):
+            raw[name] = keep.tile([P, 4, M], F32, name="raw_" + name)
+            nc.sync.dma_start(raw[name][:], w.rearrange("(p j) m -> p j m", j=4))
+
+        table_scales = keep.tile([P, T], U8, name="table_scales", align_bytes=64)
+        nc.vector.memset(table_scales[:].bitcast(I32), 0)
+        for q in range(4):
+            nc.scalar.dma_start(table_scales[32 * q : 32 * q + 4, :].bitcast(I32), x_scales[0, 4 * q : 4 * q + 4, :].bitcast(I32))
+
+        identity = keep.tile([P, P], F32, name="identity")
+        make_identity(nc, identity[:])
+
+        picked_scales = keep.tile([P, S], U8, name="picked_scales", align_bytes=64)
+        nc.vector.tensor_copy(picked_scales[:], table_scales[:].indirect(offsets[:]))
+        x_sc = keep.tile([P, HALVES, D, P], U8, name="x_sc", align_bytes=64)
+        nc.vector.tensor_copy(x_sc[:], picked_scales[:].rearrange("p (b v d) -> p b d v", b=HALVES, d=D))
+
+        x_cd = []
+        for vb in range(HALVES):
+            codes = keep.tile([P, D, P], U32, name="x_cd%d" % vb, align_bytes=64)
+            nc.vector.tensor_copy(codes[:].rearrange("p d v -> p v d"), table_words[:].indirect(offsets[:, 32 * vb : 32 * (vb + 1)]))
+            x_cd.append(codes)
+
+        u_bank = psum.tile([P, HALVES, M], F32, name="u_bank", tag="h3")
+        for vb in range(HALVES):
+            for mh in range(HALVES):
+                nc.tensor.transpose(u_bank[:, vb, mh * P : (mh + 1) * P], u_rows[:, mh, vb * P : (vb + 1) * P], identity[:])
+        u_turned = keep.tile([P, HALVES, M], F32, name="u_turned")
+        nc.scalar.activation(u_turned[:], u_bank[:], ACT.Copy, scale=1.25)
+
+        w_cd, w_sc = {}, {}
+        for name in ("g", "h"):
+            grouped = keep.tile([P, M, 4], BF16, name="grouped_" + name, align_bytes=64)
+            nc.scalar.copy(
+                grouped[:].rearrange("p (c i) j -> p c j i", i=4),
+                raw[name][:].rearrange("p j (c i) -> p c j i", i=4),
+            )
+            w_cd[name] = keep.tile([P, M], U32, name="w_cd_" + name, align_bytes=64)
+            w_sc[name] = keep.tile([P, M], U8, name="w_sc_" + name, align_bytes=64)
+            nc.vector.quantize_mx(out=w_cd[name][:].bitcast(FP8X4), scales=w_sc[name][:], in_=grouped[:].rearrange("p m j -> p (m j)"))
+
+        def product(name, c):
+            vb, mh = chunks[c]
+            bank = psum.tile([P, D, P], F32, name="y%s%d" % (name, c), tag="%s%d" % (name, c))
+            cols = slice(mh * P, (mh + 1) * P)
+            for d in range(D):
+                nc.tensor.matmul_mx(
+                    out=bank[:, d, :],
+                    lhsT=x_cd[vb][:, d, :].bitcast(FP8X4),
+                    lhsT_scale=x_sc[:, vb, d, :],
+                    rhs=w_cd[name][:, cols].bitcast(FP8X4),
+                    rhs_scale=w_sc[name][:, cols],
+                    start=True,
+                    stop=True,
+                )
+            return bank
+
+        def sum_turned(dst, src):
+            for d in range(D):
+                nc.tensor.matmul(dst, lhsT=src[:, d, :], rhs=identity[:], is_transpose=True, start=(d == 0), stop=(d == D - 1))
+
+        def wide(name):
+            return [keep.tile([P, D, P], F32, name="%s%d" % (name, c)) for c in range(n_chunks)]
+
+        yg, yh = [], []
+        for c in range(n_chunks):
+            yg.append(product("g", c))
+            yh.append(product("h", c))
+
+        tilt, bar, slack, ws, sq, q2, push, pw, wk = (wide(n) for n in ("tilt", "bar", "slack", "ws", "sq", "q2", "push", "pw", "wk"))
+        gap = keep.tile([P, n_chunks, D, P], F32, name="gap", tag="gap_then_rq")
+        for c, (vb, mh) in enumerate(chunks):
+            u_c = u_turned[:, vb, mh * P : (mh + 1) * P].unsqueeze(1).to_broadcast([P, D, P])
+            nc.scalar.activation(bar[c][:], yh[c][:], ACT.Exp, scale=0.4)
+            nc.vector.tensor_tensor(tilt[c][:], yg[c][:], u_c, ALU.mult)
+            nc.vector.scalar_tensor_tensor(slack[c][:], bar[c][:], 1.0, tilt[c][:], ALU.subtract, ALU.add)
+            pair = keep.tile([P, 2, P], F32, name="pair%d" % c)
+            nc.vector.tensor_tensor(pair[:], slack[c][:, 0:2, :], slack[c][:, 2:4, :], ALU.min)
+            worst = keep.tile([P, P], F32, name="worst%d" % c)
+            nc.vector.tensor_tensor(worst[:], pair[:, 0, :], pair[:, 1, :], ALU.min)
+            nc.vector.tensor_tensor(gap[:, c], worst[:].unsqueeze(1).to_broadcast([P, D, P]), slack[c][:], ALU.subtract)
+            nc.scalar.activation(ws[c][:], gap[:, c], ACT.Exp, scale=4.0)
+
+        den = psum.tile([P, n_chunks, P], F32, name="den", tag="h0")
+        for c in range(n_chunks):
+            nc.scalar.activation(sq[c][:], yg[c][:], ACT.Square)
+            nc.scalar.activation(q2[c][:], sq[c][:], ACT.Square, scale=SHRINK / 0.3, bias=SHRINK)
+            sum_turned(den[:, c, :], ws[c])
+            nc.vector.scalar_tensor_tensor(push[c][:], slack[c][:], 0.0, yg[c][:], ALU.min, ALU.mult)
+            nc.vector.tensor_tensor(pw[c][:], push[c][:], ws[c][:], ALU.mult)
+
+        rq = keep.tile([P, n_chunks, D, P], F32, name="rq", tag="gap_then_rq")
+        for c in range(n_chunks):
+            nc.scalar.activation(rq[:, c], q2[c][:], ACT.Abs_reciprocal_sqrt)
+        den2 = keep.tile([P, n_chunks, P], F32, name="den2")
+        nc.scalar.activation(den2[:], den[:], ACT.Square)
+        rden = keep.tile([P, n_chunks, P], F32, name="rden")
+        nc.scalar.activation(rden[:], den2[:], ACT.Abs_reciprocal_sqrt)
+
+        num_tags = ("h1", "h2", "h3", "g0")
+        for c, (vb, mh) in enumerate(chunks):
+            nc.vector.tensor_tensor(wk[c][:], pw[c][:], rq[:, c], ALU.mult)
+            num = psum.tile([P, P], F32, name="num%d" % c, tag=num_tags[c])
+            sum_turned(num[:], wk[c])
+            repair = keep.tile([P, P], F32, name="repair%d" % c)
+            nc.vector.scalar_tensor_tensor(repair[:], num[:], -0.8 * SHRINK / 0.3, rden[:, c, :], ALU.mult, ALU.mult)
+            result = keep.tile([P, P], F32, name="result%d" % c)
+            nc.vector.tensor_tensor(result[:], repair[:], u_rows[:, mh, vb * P : (vb + 1) * P], ALU.add)
+            nc.sync.dma_start(out[mh * P : (mh + 1) * P, vb * P : (vb + 1) * P], result[:])

@@ -16,34 +16,37 @@ ACT = mybir.ActivationFunctionType
 P = 128
 K, T, S, D, M, V = 512, 4096, 1024, 4, 256, 256
 HALVES = 2
-CHUNK = D * P
 FLOPS = 2 * 2 * K * M * S
 SHRINK = 2.0 ** -24
+SPLIT = 640
+HEAD = 512
 
 
 def tile_picked_ycbf_worst_p_kernel(tc, x_words, x_scales, w1, w2, unom, offs, out):
     nc = tc.nc
-    chunks = [(vb, mh) for vb in range(HALVES) for mh in range(HALVES)]
-    n_chunks = len(chunks)
+    halves = range(HALVES)
+    pieces = [(vb, mh) for vb in halves for mh in halves]
+    n_pieces = len(pieces)
     with ExitStack() as ctx:
         keep = ctx.enter_context(tc.tile_pool(name="keep", bufs=1))
         psum = ctx.enter_context(tc.psum_pool(name="psum", bufs=1))
 
         offsets = keep.tile([P, S // 16], U16, name="offsets")
         nc.sync.dma_start(offsets[:], offs)
-        u_rows = keep.tile([P, HALVES, V], F32, name="u_rows")
-        nc.sync.dma_start(u_rows[:], unom.rearrange("(h p) v -> p h v", p=P))
-        table_words = keep.tile([P, T], U32, name="table_words", align_bytes=64)
-        nc.sync.dma_start(table_words[:].bitcast(I32), x_words[0].rearrange("p n t -> p (n t)").bitcast(I32))
-        raw = {}
-        for name, w in (("g", w2), ("h", w1)):
-            raw[name] = keep.tile([P, 4, M], F32, name="raw_" + name)
-            nc.sync.dma_start(raw[name][:], w.rearrange("(p j) m -> p j m", j=4))
-
         table_scales = keep.tile([P, T], U8, name="table_scales", align_bytes=64)
-        nc.vector.memset(table_scales[:].bitcast(I32), 0)
-        for q in range(4):
-            nc.scalar.dma_start(table_scales[32 * q : 32 * q + 4, :].bitcast(I32), x_scales[0, 4 * q : 4 * q + 4, :].bitcast(I32))
+        nc.vector.memset(table_scales[:].bitcast(I32)[:, :SPLIT], 0)
+        nc.gpsimd.memset(table_scales[:].bitcast(I32)[:, SPLIT:], 0)
+        table_words = keep.tile([P, T], U32, name="table_words", align_bytes=64)
+        words_hbm = x_words[0].rearrange("p n t -> p (n t)").bitcast(I32)
+        nc.sync.dma_start(table_words[:, :HEAD].bitcast(I32), words_hbm[:, :HEAD])
+        for r in range(4):
+            nc.sync.dma_start(table_scales[r:P:32, :].bitcast(I32), x_scales[0, r:16:4, :].bitcast(I32))
+        nc.sync.dma_start(table_words[:, HEAD:].bitcast(I32), words_hbm[:, HEAD:])
+        raw = {name: keep.tile([P, 4, M], F32, name="raw_" + name, tag="raw_" + name) for name in ("g", "h")}
+        u_rows = keep.tile([P, HALVES, V], F32, name="u_rows")
+        nc.sync.dma_start(raw["g"][:], w2.rearrange("(p j) m -> p j m", j=4))
+        nc.sync.dma_start(u_rows[:], unom.rearrange("(h p) v -> p h v", p=P))
+        nc.sync.dma_start(raw["h"][:], w1.rearrange("(p j) m -> p j m", j=4))
 
         identity = keep.tile([P, P], F32, name="identity")
         make_identity(nc, identity[:])
@@ -53,41 +56,50 @@ def tile_picked_ycbf_worst_p_kernel(tc, x_words, x_scales, w1, w2, unom, offs, o
         x_sc = keep.tile([P, HALVES, D, P], U8, name="x_sc", align_bytes=64)
         nc.vector.tensor_copy(x_sc[:], picked_scales[:].rearrange("p (b v d) -> p b d v", b=HALVES, d=D))
 
-        x_cd = []
-        for vb in range(HALVES):
-            codes = keep.tile([P, D, P], U32, name="x_cd%d" % vb, align_bytes=64)
-            nc.vector.tensor_copy(codes[:].rearrange("p d v -> p v d"), table_words[:].indirect(offsets[:, 32 * vb : 32 * (vb + 1)]))
-            x_cd.append(codes)
-
-        u_bank = psum.tile([P, HALVES, M], F32, name="u_bank", tag="h3")
-        for vb in range(HALVES):
-            for mh in range(HALVES):
-                nc.tensor.transpose(u_bank[:, vb, mh * P : (mh + 1) * P], u_rows[:, mh, vb * P : (vb + 1) * P], identity[:])
-        u_turned = keep.tile([P, HALVES, M], F32, name="u_turned")
-        nc.scalar.activation(u_turned[:], u_bank[:], ACT.Copy, scale=1.25)
-
         w_cd, w_sc = {}, {}
-        for name in ("g", "h"):
-            grouped = keep.tile([P, M, 4], BF16, name="grouped_" + name, align_bytes=64)
+
+        def quantize(name, mh):
+            grouped = keep.tile([P, P, 4], BF16, name="grouped_%s%d" % (name, mh), tag="grouped_%s%d" % (name, mh), align_bytes=64)
             nc.scalar.copy(
                 grouped[:].rearrange("p (c i) j -> p c j i", i=4),
-                raw[name][:].rearrange("p j (c i) -> p c j i", i=4),
+                raw[name][:, :, mh * P : (mh + 1) * P].rearrange("p j (c i) -> p c j i", i=4),
             )
-            w_cd[name] = keep.tile([P, M], U32, name="w_cd_" + name, align_bytes=64)
-            w_sc[name] = keep.tile([P, M], U8, name="w_sc_" + name, align_bytes=64)
-            nc.vector.quantize_mx(out=w_cd[name][:].bitcast(FP8X4), scales=w_sc[name][:], in_=grouped[:].rearrange("p m j -> p (m j)"))
+            w_cd[name, mh] = keep.tile([P, P], U32, name="w_cd_%s%d" % (name, mh), align_bytes=64)
+            w_sc[name, mh] = keep.tile([P, P], U8, name="w_sc_%s%d" % (name, mh), align_bytes=64)
+            nc.vector.quantize_mx(out=w_cd[name, mh][:].bitcast(FP8X4), scales=w_sc[name, mh][:], in_=grouped[:].rearrange("p m j -> p (m j)"))
+
+        for mh in halves:
+            quantize("g", mh)
+        u_bank = psum.tile([P, n_pieces, P], F32, name="u_bank", tag="h3")
+        for c, (vb, mh) in enumerate(pieces):
+            nc.tensor.transpose(u_bank[:, c, :], u_rows[:, mh, vb * P : (vb + 1) * P], identity[:])
+        u_turned = keep.tile([P, n_pieces, P], F32, name="u_turned")
+        nc.scalar.activation(u_turned[:], u_bank[:], ACT.Copy, scale=1.25)
+
+        for mh in halves:
+            quantize("h", mh)
+
+        x_cd = []
+        for vb in halves:
+            picked = keep.tile([P, D * P], U32, name="picked%d" % vb, tag=("picked", "grouped_g0")[vb], align_bytes=64)
+            nc.vector.tensor_copy(picked[:], table_words[:].indirect(offsets[:, 32 * vb : 32 * (vb + 1)]))
+            codes = keep.tile([P, D, P], U32, name="x_cd%d" % vb, align_bytes=64)
+            nc.vector.tensor_copy(
+                codes[:].rearrange("p d (c i) -> p c d i", i=4),
+                picked[:].rearrange("p (c i d) -> p c d i", i=4, d=D),
+            )
+            x_cd.append(codes)
 
         def product(name, c):
-            vb, mh = chunks[c]
+            vb, mh = pieces[c]
             bank = psum.tile([P, D, P], F32, name="y%s%d" % (name, c), tag="%s%d" % (name, c))
-            cols = slice(mh * P, (mh + 1) * P)
             for d in range(D):
                 nc.tensor.matmul_mx(
                     out=bank[:, d, :],
                     lhsT=x_cd[vb][:, d, :].bitcast(FP8X4),
                     lhsT_scale=x_sc[:, vb, d, :],
-                    rhs=w_cd[name][:, cols].bitcast(FP8X4),
-                    rhs_scale=w_sc[name][:, cols],
+                    rhs=w_cd[name, mh][:].bitcast(FP8X4),
+                    rhs_scale=w_sc[name, mh][:],
                     start=True,
                     stop=True,
                 )
@@ -97,51 +109,62 @@ def tile_picked_ycbf_worst_p_kernel(tc, x_words, x_scales, w1, w2, unom, offs, o
             for d in range(D):
                 nc.tensor.matmul(dst, lhsT=src[:, d, :], rhs=identity[:], is_transpose=True, start=(d == 0), stop=(d == D - 1))
 
-        def wide(name):
-            return [keep.tile([P, D, P], F32, name="%s%d" % (name, c)) for c in range(n_chunks)]
+        def wide(name, tag=None):
+            return keep.tile([P, n_pieces, D, P], F32, name=name, tag=tag or name, align_bytes=64)
 
         yg, yh = [], []
-        for c in range(n_chunks):
+        for c in range(n_pieces):
             yg.append(product("g", c))
             yh.append(product("h", c))
 
-        tilt, bar, slack, ws, sq, q2, push, pw, wk = (wide(n) for n in ("tilt", "bar", "slack", "ws", "sq", "q2", "push", "pw", "wk"))
-        gap = keep.tile([P, n_chunks, D, P], F32, name="gap", tag="gap_then_rq")
-        for c, (vb, mh) in enumerate(chunks):
-            u_c = u_turned[:, vb, mh * P : (mh + 1) * P].unsqueeze(1).to_broadcast([P, D, P])
-            nc.scalar.activation(bar[c][:], yh[c][:], ACT.Exp, scale=0.4)
-            nc.vector.tensor_tensor(tilt[c][:], yg[c][:], u_c, ALU.mult)
-            nc.vector.scalar_tensor_tensor(slack[c][:], bar[c][:], 1.0, tilt[c][:], ALU.subtract, ALU.add)
-            pair = keep.tile([P, 2, P], F32, name="pair%d" % c)
-            nc.vector.tensor_tensor(pair[:], slack[c][:, 0:2, :], slack[c][:, 2:4, :], ALU.min)
-            worst = keep.tile([P, P], F32, name="worst%d" % c)
-            nc.vector.tensor_tensor(worst[:], pair[:, 0, :], pair[:, 1, :], ALU.min)
-            nc.vector.tensor_tensor(gap[:, c], worst[:].unsqueeze(1).to_broadcast([P, D, P]), slack[c][:], ALU.subtract)
-            nc.scalar.activation(ws[c][:], gap[:, c], ACT.Exp, scale=4.0)
+        bar, slack, ws, q2, push, pw, wk = (wide(n) for n in ("bar", "slack", "ws", "q2", "push", "pw", "wk"))
+        tilt = wide("tilt", None)
+        gap = wide("gap", "gap_then_rq")
+        pair = keep.tile([P, n_pieces, 2, P], F32, name="pair")
+        worst = keep.tile([P, n_pieces, P], F32, name="worst")
+        for group in ((0,), (1,), (2, 3)):
+            cs = slice(group[0], group[-1] + 1)
+            for c in group:
+                nc.scalar.activation(bar[:, c], yh[c][:], ACT.Exp, scale=0.4)
+                nc.vector.tensor_tensor(tilt[:, c], yg[c][:], u_turned[:, c, :].unsqueeze(1).to_broadcast([P, D, P]), ALU.mult)
+            nc.vector.scalar_tensor_tensor(slack[:, cs], bar[:, cs], 1.0, tilt[:, cs], ALU.subtract, ALU.add)
+            nc.vector.tensor_tensor(pair[:, cs], slack[:, cs, 0:2, :], slack[:, cs, 2:4, :], ALU.min)
+            nc.vector.tensor_tensor(worst[:, cs, :], pair[:, cs, 0, :], pair[:, cs, 1, :], ALU.min)
+            for c in group:
+                nc.vector.tensor_tensor(gap[:, c], worst[:, c, :].unsqueeze(1).to_broadcast([P, D, P]), slack[:, c], ALU.subtract)
+                nc.scalar.activation(ws[:, c], gap[:, c], ACT.Exp, scale=4.0)
 
-        den = psum.tile([P, n_chunks, P], F32, name="den", tag="h0")
-        for c in range(n_chunks):
-            nc.scalar.activation(sq[c][:], yg[c][:], ACT.Square)
-            nc.scalar.activation(q2[c][:], sq[c][:], ACT.Square, scale=SHRINK / 0.3, bias=SHRINK)
-            sum_turned(den[:, c, :], ws[c])
-            nc.vector.scalar_tensor_tensor(push[c][:], slack[c][:], 0.0, yg[c][:], ALU.min, ALU.mult)
-            nc.vector.tensor_tensor(pw[c][:], push[c][:], ws[c][:], ALU.mult)
+        den = [psum.tile([P, HALVES, P], F32, name="den%d" % vb, tag="h%d" % vb) for vb in halves]
+        den2 = keep.tile([P, HALVES, HALVES, P], F32, name="den2")
+        for vb in halves:
+            cs = slice(HALVES * vb, HALVES * (vb + 1))
+            sq = keep.tile([P, HALVES, D, P], F32, name="sq%d" % vb, tag="raw_h")
+            for mh in halves:
+                c = HALVES * vb + mh
+                nc.scalar.activation(sq[:, mh], yg[c][:], ACT.Square)
+                nc.vector.scalar_tensor_tensor(push[:, c], slack[:, c], 0.0, yg[c][:], ALU.min, ALU.mult)
+                sum_turned(den[vb][:, mh, :], ws[:, c])
+            nc.scalar.activation(q2[:, cs], sq[:], ACT.Square, scale=SHRINK / 0.3, bias=SHRINK)
+            nc.vector.tensor_tensor(pw[:, cs], push[:, cs], ws[:, cs], ALU.mult)
 
-        rq = keep.tile([P, n_chunks, D, P], F32, name="rq", tag="gap_then_rq")
-        for c in range(n_chunks):
-            nc.scalar.activation(rq[:, c], q2[c][:], ACT.Abs_reciprocal_sqrt)
-        den2 = keep.tile([P, n_chunks, P], F32, name="den2")
-        nc.scalar.activation(den2[:], den[:], ACT.Square)
-        rden = keep.tile([P, n_chunks, P], F32, name="rden")
-        nc.scalar.activation(rden[:], den2[:], ACT.Abs_reciprocal_sqrt)
+        rq = wide("rq", "gap_then_rq")
+        rden = keep.tile([P, HALVES, HALVES, P], F32, name="rden")
+        nc.scalar.activation(den2[:, 0], den[0][:], ACT.Square)
+        for c in range(n_pieces):
+            nc.scalar.activation(rq[:, c], q2[:, c], ACT.Abs_reciprocal_sqrt)
+            if c == 1:
+                nc.scalar.activation(den2[:, 1], den[1][:], ACT.Square)
+                nc.scalar.activation(rden[:], den2[:], ACT.Abs_reciprocal_sqrt)
 
-        num_tags = ("h1", "h2", "h3", "g0")
-        for c, (vb, mh) in enumerate(chunks):
-            nc.vector.tensor_tensor(wk[c][:], pw[c][:], rq[:, c], ALU.mult)
-            num = psum.tile([P, P], F32, name="num%d" % c, tag=num_tags[c])
-            sum_turned(num[:], wk[c])
+        num_tags = ("h2", "h3", "g0", "g1")
+        num = []
+        for c in range(n_pieces):
+            nc.vector.tensor_tensor(wk[:, c], pw[:, c], rq[:, c], ALU.mult)
+            num.append(psum.tile([P, P], F32, name="num%d" % c, tag=num_tags[c]))
+            sum_turned(num[c][:], wk[:, c])
+        for c, (vb, mh) in enumerate(pieces):
             repair = keep.tile([P, P], F32, name="repair%d" % c)
-            nc.vector.scalar_tensor_tensor(repair[:], num[:], -0.8 * SHRINK / 0.3, rden[:, c, :], ALU.mult, ALU.mult)
+            nc.vector.scalar_tensor_tensor(repair[:], num[c][:], -0.8 * SHRINK / 0.3, rden[:, vb, mh, :], ALU.mult, ALU.mult)
             result = keep.tile([P, P], F32, name="result%d" % c)
             nc.vector.tensor_tensor(result[:], repair[:], u_rows[:, mh, vb * P : (vb + 1) * P], ALU.add)
             nc.sync.dma_start(out[mh * P : (mh + 1) * P, vb * P : (vb + 1) * P], result[:])

from contextlib import ExitStack

import concourse.mybir as mybir
from concourse.masks import make_identity

F32 = mybir.dt.float32
BF16 = mybir.dt.bfloat16
I32 = mybir.dt.int32
U32 = mybir.dt.uint32
U16 = mybir.dt.uint16
U8 = mybir.dt.uint8
FP8X4 = mybir.dt.float8_e4m3fn_x4
ALU = mybir.AluOpType
ACT = mybir.ActivationFunctionType

P = 128
K, T, S, D, M, V = 512, 4096, 1024, 4, 256, 256
HALVES = 2
FLOPS = 2 * 2 * K * M * S
SHRINK = 2.0 ** -24
SPLIT = 640
HEAD = 512


def tile_picked_ycbf_worst_p_kernel(tc, x_words, x_scales, w1, w2, unom, offs, out):
    nc = tc.nc
    halves = range(HALVES)
    pieces = [(vb, mh) for vb in halves for mh in halves]
    n_pieces = len(pieces)
    with ExitStack() as ctx:
        keep = ctx.enter_context(tc.tile_pool(name="keep", bufs=1))
        psum = ctx.enter_context(tc.psum_pool(name="psum", bufs=1))

        offsets = keep.tile([P, S // 16], U16, name="offsets")
        nc.sync.dma_start(offsets[:], offs)
        table_scales = keep.tile([P, T], U8, name="table_scales", align_bytes=64)
        nc.vector.memset(table_scales[:].bitcast(I32)[:, :SPLIT], 0)
        nc.gpsimd.memset(table_scales[:].bitcast(I32)[:, SPLIT:], 0)
        table_words = keep.tile([P, T], U32, name="table_words", align_bytes=64)
        words_hbm = x_words[0].rearrange("p n t -> p (n t)").bitcast(I32)
        nc.sync.dma_start(table_words[:, :HEAD].bitcast(I32), words_hbm[:, :HEAD])
        for r in range(4):
            nc.sync.dma_start(table_scales[r:P:32, :].bitcast(I32), x_scales[0, r:16:4, :].bitcast(I32))
        nc.sync.dma_start(table_words[:, HEAD:].bitcast(I32), words_hbm[:, HEAD:])
        raw = {name: keep.tile([P, 4, M], F32, name="raw_" + name, tag="raw_" + name) for name in ("g", "h")}
        u_rows = keep.tile([P, HALVES, V], F32, name="u_rows")
        nc.sync.dma_start(raw["g"][:], w2.rearrange("(p j) m -> p j m", j=4))
        nc.sync.dma_start(u_rows[:], unom.rearrange("(h p) v -> p h v", p=P))
        nc.sync.dma_start(raw["h"][:], w1.rearrange("(p j) m -> p j m", j=4))

        identity = keep.tile([P, P], F32, name="identity")
        make_identity(nc, identity[:])

        picked_scales = keep.tile([P, S], U8, name="picked_scales", align_bytes=64)
        nc.vector.tensor_copy(picked_scales[:], table_scales[:].indirect(offsets[:]))
        x_sc = keep.tile([P, HALVES, D, P], U8, name="x_sc", align_bytes=64)
        nc.vector.tensor_copy(x_sc[:], picked_scales[:].rearrange("p (b v d) -> p b d v", b=HALVES, d=D))

        w_cd, w_sc = {}, {}

        def quantize(name, mh):
            grouped = keep.tile([P, P, 4], BF16, name="grouped_%s%d" % (name, mh), tag="grouped_%s%d" % (name, mh), align_bytes=64)
            nc.scalar.copy(
                grouped[:].rearrange("p (c i) j -> p c j i", i=4),
                raw[name][:, :, mh * P : (mh + 1) * P].rearrange("p j (c i) -> p c j i", i=4),
            )
            w_cd[name, mh] = keep.tile([P, P], U32, name="w_cd_%s%d" % (name, mh), align_bytes=64)
            w_sc[name, mh] = keep.tile([P, P], U8, name="w_sc_%s%d" % (name, mh), align_bytes=64)
            nc.vector.quantize_mx(out=w_cd[name, mh][:].bitcast(FP8X4), scales=w_sc[name, mh][:], in_=grouped[:].rearrange("p m j -> p (m j)"))

        for mh in halves:
            quantize("g", mh)
        u_bank = psum.tile([P, n_pieces, P], F32, name="u_bank", tag="h3")
        for c, (vb, mh) in enumerate(pieces):
            nc.tensor.transpose(u_bank[:, c, :], u_rows[:, mh, vb * P : (vb + 1) * P], identity[:])
        u_turned = keep.tile([P, n_pieces, P], F32, name="u_turned")
        nc.scalar.activation(u_turned[:], u_bank[:], ACT.Copy, scale=1.25)

        for mh in halves:
            quantize("h", mh)

        x_cd = []
        for vb in halves:
            picked = keep.tile([P, D * P], U32, name="picked%d" % vb, tag=("picked", "grouped_g0")[vb], align_bytes=64)
            nc.vector.tensor_copy(picked[:], table_words[:].indirect(offsets[:, 32 * vb : 32 * (vb + 1)]))
            codes = keep.tile([P, D, P], U32, name="x_cd%d" % vb, align_bytes=64)
            nc.vector.tensor_copy(
                codes[:].rearrange("p d (c i) -> p c d i", i=4),
                picked[:].rearrange("p (c i d) -> p c d i", i=4, d=D),
            )
            x_cd.append(codes)

        def product(name, c):
            vb, mh = pieces[c]
            bank = psum.tile([P, D, P], F32, name="y%s%d" % (name, c), tag="%s%d" % (name, c))
            for d in range(D):
                nc.tensor.matmul_mx(
                    out=bank[:, d, :],
                    lhsT=x_cd[vb][:, d, :].bitcast(FP8X4),
                    lhsT_scale=x_sc[:, vb, d, :],
                    rhs=w_cd[name, mh][:].bitcast(FP8X4),
                    rhs_scale=w_sc[name, mh][:],
                    start=True,
                    stop=True,
                )
            return bank

        def sum_turned(dst, src):
            for d in range(D):
                nc.tensor.matmul(dst, lhsT=src[:, d, :], rhs=identity[:], is_transpose=True, start=(d == 0), stop=(d == D - 1))

        def wide(name, tag=None):
            return keep.tile([P, n_pieces, D, P], F32, name=name, tag=tag or name, align_bytes=64)

        yg, yh = [], []
        for c in range(n_pieces):
            yg.append(product("g", c))
            yh.append(product("h", c))

        bar, slack, ws, q2, push, pw, wk = (wide(n) for n in ("bar", "slack", "ws", "q2", "push", "pw", "wk"))
        tilt = wide("tilt", None)
        gap = wide("gap", "gap_then_rq")
        pair = keep.tile([P, n_pieces, 2, P], F32, name="pair")
        worst = keep.tile([P, n_pieces, P], F32, name="worst")
        for group in ((0,), (1,), (2, 3)):
            cs = slice(group[0], group[-1] + 1)
            for c in group:
                nc.scalar.activation(bar[:, c], yh[c][:], ACT.Exp, scale=0.4)
                nc.vector.tensor_tensor(tilt[:, c], yg[c][:], u_turned[:, c, :].unsqueeze(1).to_broadcast([P, D, P]), ALU.mult)
            nc.vector.scalar_tensor_tensor(slack[:, cs], bar[:, cs], 1.0, tilt[:, cs], ALU.subtract, ALU.add)
            nc.vector.tensor_tensor(pair[:, cs], slack[:, cs, 0:2, :], slack[:, cs, 2:4, :], ALU.min)
            nc.vector.tensor_tensor(worst[:, cs, :], pair[:, cs, 0, :], pair[:, cs, 1, :], ALU.min)
            for c in group:
                nc.vector.tensor_tensor(gap[:, c], worst[:, c, :].unsqueeze(1).to_broadcast([P, D, P]), slack[:, c], ALU.subtract)
                nc.scalar.activation(ws[:, c], gap[:, c], ACT.Exp, scale=4.0)

        den = [psum.tile([P, HALVES, P], F32, name="den%d" % vb, tag="h%d" % vb) for vb in halves]
        den2 = keep.tile([P, HALVES, HALVES, P], F32, name="den2")
        for vb in halves:
            cs = slice(HALVES * vb, HALVES * (vb + 1))
            sq = keep.tile([P, HALVES, D, P], F32, name="sq%d" % vb, tag="raw_h")
            for mh in halves:
                c = HALVES * vb + mh
                nc.scalar.activation(sq[:, mh], yg[c][:], ACT.Square)
                nc.vector.scalar_tensor_tensor(push[:, c], slack[:, c], 0.0, yg[c][:], ALU.min, ALU.mult)
                sum_turned(den[vb][:, mh, :], ws[:, c])
            nc.scalar.activation(q2[:, cs], sq[:], ACT.Square, scale=SHRINK / 0.3, bias=SHRINK)
            nc.vector.tensor_tensor(pw[:, cs], push[:, cs], ws[:, cs], ALU.mult)

        rq = wide("rq", "gap_then_rq")
        rden = keep.tile([P, HALVES, HALVES, P], F32, name="rden")
        nc.scalar.activation(den2[:, 0], den[0][:], ACT.Square)
        for c in range(n_pieces):
            nc.scalar.activation(rq[:, c], q2[:, c], ACT.Abs_reciprocal_sqrt)
            if c == 1:
                nc.scalar.activation(den2[:, 1], den[1][:], ACT.Square)
                nc.scalar.activation(rden[:], den2[:], ACT.Abs_reciprocal_sqrt)

        num_tags = ("h2", "h3", "g0", "g1")
        num = []
        for c in range(n_pieces):
            nc.vector.tensor_tensor(wk[:, c], pw[:, c], rq[:, c], ALU.mult)
            num.append(psum.tile([P, P], F32, name="num%d" % c, tag=num_tags[c]))
            sum_turned(num[c][:], wk[:, c])
        for c, (vb, mh) in enumerate(pieces):
            repair = keep.tile([P, P], F32, name="repair%d" % c)
            nc.vector.scalar_tensor_tensor(repair[:], num[c][:], -0.8 * SHRINK / 0.3, rden[:, vb, mh, :], ALU.mult, ALU.mult)
            result = keep.tile([P, P], F32, name="result%d" % c)
            nc.vector.tensor_tensor(result[:], repair[:], u_rows[:, mh, vb * P : (vb + 1) * P], ALU.add)
            nc.sync.dma_start(out[mh * P : (mh + 1) * P, vb * P : (vb + 1) * P], result[:])
